import numpy as np
import ml_dtypes


def mxq(x, axis, fmt="e4m3"):
    dtype, down = {"e4m3": (ml_dtypes.float8_e4m3fn, 7), "e5m2": (ml_dtypes.float8_e5m2, 14)}[fmt]
    v = np.moveaxis(np.asarray(x, np.float32).astype(ml_dtypes.bfloat16).astype(np.float64), axis, -1)
    blocks = v.reshape(v.shape[:-1] + (-1, 32))
    amax = np.abs(blocks).max(-1, keepdims=True)
    byte = np.maximum(np.where(amax > 0, np.frexp(amax)[1] - 1 + 127, 0) - down, 1)
    scale = np.exp2(byte - 127.0)
    codes = (blocks / scale).astype(np.float32).astype(dtype).astype(np.float64)
    return np.moveaxis((codes * scale).reshape(v.shape), -1, axis)


WIDE = False


def mx_kscale(k):
    if not WIDE:
        return np.ones(k)
    levels = np.array([30, -30])
    if k % 512:
        return np.exp2(np.random.permutation(np.resize(levels, k // 32))).repeat(32)
    a = np.empty((k // 512, 16))
    for p in range(k // 512):
        a[p, :8] = np.random.permutation(np.resize(levels, 8))
        for g in range(8):
            far = levels[np.abs(levels - a[p, g]) >= 10]
            a[p, g + 8] = far[np.random.randint(len(far))]
    return np.exp2(a.ravel()).repeat(32)


def f64(x):
    return np.asarray(x).astype(np.float64)


E2M1 = np.array([0.0, 0.5, 1.0, 1.5, 2.0, 3.0, 4.0, 6.0, -0.0, -0.5, -1.0, -1.5, -2.0, -3.0, -4.0, -6.0])


def pack_weight(w, fmt):
    k, n = w.shape
    w = f64(np.asarray(w, np.float32).astype(ml_dtypes.bfloat16)).reshape(k // 32, 32, n)
    amax = np.abs(w).max(1)
    if fmt == "e4m3":
        byte = np.frexp(amax)[1] - 1 + 127 - 7
    else:
        mant, ex = np.frexp(amax / 6.0)
        byte = np.where(mant > 0.5, ex, ex - 1) + 127
    byte = np.clip(np.where(amax > 0, byte, 1), 1, 254)
    scaled = (w * np.exp2(127.0 - byte)[:, None, :]).reshape(k, n).astype(np.float32)
    by_word = np.ascontiguousarray(scaled.reshape(k // 512, 128, 4, n).transpose(0, 1, 3, 2))
    if fmt == "e4m3":
        words = by_word.astype(ml_dtypes.float8_e4m3fn).view(np.uint8)
    else:
        c = by_word.astype(ml_dtypes.float4_e2m1fn).view(np.uint8) & 0xF
        words = (c[..., 0::2] | (c[..., 1::2] << 4)).reshape(k // 512, 128, 2 * n)
    return np.ascontiguousarray(words), np.ascontiguousarray(byte.astype(np.uint8).reshape(k // 512, 16, n))


def unpack_weight(words, scales, fmt):
    g, _, n = scales.shape
    words = np.ascontiguousarray(words).reshape(g, 128, n, -1)
    if fmt == "e4m3":
        vals = words.view(ml_dtypes.float8_e4m3fn).astype(np.float64)
    else:
        nib = np.empty((g, 128, n, 4), np.uint8)
        nib[..., 0::2] = words & 0xF
        nib[..., 1::2] = words >> 4
        vals = E2M1[nib]
    vals = vals * np.repeat(np.exp2(scales.astype(np.float64) - 127.0), 8, axis=1)[..., None]
    return vals.transpose(0, 1, 3, 2).reshape(g * 512, n)


K, L, R, M, T = 512, 1536, 1024, 1536, 1024


def setup_inputs():
    n = np.random.standard_normal
    s1 = mx_kscale(K)[:, None]
    s2 = mx_kscale(L)[:, None]
    u = mx_kscale(R)[:, None]
    p_w = pack_weight(n((R, M)) / np.sqrt(R) / u, "e2m1")
    return {
        "x": (n((K, T)) * s1).astype(np.float32),
        "wx": (n((K, R)) / np.sqrt(K) / s1 * u.T).astype(np.float32),
        "c": (n((L, T)) * s2).astype(np.float32),
        "wc": (n((L, R)) / np.sqrt(L) / s2).astype(np.float32),
        "w_words": p_w[0],
        "w_scales": p_w[1],
        "b": (0.3 * n(1536)).astype(np.float32),
    }


def reference(x, wx, c, wc, w_words, w_scales, b):
    x_ = mxq(f64(x), 0, "e4m3")
    wx_ = mxq(f64(wx), 0, "e4m3")
    c_ = mxq(f64(c), 0, "e5m2")
    wc_ = mxq(f64(wc), 0, "e4m3")
    w_ = unpack_weight(w_words, w_scales, "e2m1")
    h_ = mxq((wx_.T @ x_) * (wc_.T @ c_), 0, "e4m3")
    y = w_.T @ h_
    return y + f64(b)[:, None]

from contextlib import ExitStack

import concourse.mybir as mybir
from concourse.masks import make_identity

K, L, R, M, T = 512, 1536, 1024, 1536, 1024
FLOPS = 2 * T * R * (K + L + M)

F32 = mybir.dt.float32
BF16 = mybir.dt.bfloat16
I32 = mybir.dt.int32
U32 = mybir.dt.uint32
U8 = mybir.dt.uint8
E4M3 = mybir.dt.float8_e4m3fn_x4
E5M2 = mybir.dt.float8_e5m2_x4
E2M1 = mybir.dt.float4_e2m1fn_x4

P = 128
PACK = 4
PASS = P * PACK
HALF = 512
QUARTER = 128
C_PASSES = L // PASS
N_TILES = M // P
RAW_SLOTS = 8
GROUPED_SLOTS = 3
STORE_TILES = 2


def tile_mix_bilin_fm_bias_kernel(tc, x, wx, c, wc, w_words, w_scales, b, out):
    nc = tc.nc
    dram = {"x": x, "wx": wx, "c": c, "wc": wc}

    units = []
    for g in range(C_PASSES):
        units.extend([("c", g, 0), ("wc", g, 0)])
    units.extend([("x", 0, 0), ("wx", 0, 0)])
    units.extend([("wc", g, 1) for g in range(C_PASSES)])
    units.append(("wx", 0, 1))
    units.extend([("c", g, 1) for g in range(C_PASSES)])
    units.append(("x", 0, 1))

    with ExitStack() as ctx:
        sbuf = ctx.enter_context(tc.tile_pool(name="sbuf", bufs=1))
        psum = ctx.enter_context(tc.psum_pool(name="psum", bufs=1))

        raw = [sbuf.tile([P, PACK, HALF], F32, name="raw%d" % s, align_bytes=64) for s in range(RAW_SLOTS)]
        grouped = [sbuf.tile([P, PACK * HALF], BF16, name="grouped%d" % s, align_bytes=64) for s in range(GROUPED_SLOTS)]
        codes = {u: sbuf.tile([P, HALF], U32, name="codes_%s%d%d" % u, align_bytes=64) for u in units}
        scales = {u: sbuf.tile([P, HALF], U8, name="scales_%s%d%d" % u, align_bytes=64) for u in units}
        pc_sb = [sbuf.tile([P, PACK, HALF], F32, name="pc_sb%d" % a, align_bytes=64) for a in range(2)]
        h_bf = [sbuf.tile([P, PACK * HALF], BF16, name="h_bf%d" % a, align_bytes=64) for a in range(2)]
        h_codes = {(t, a): sbuf.tile([P, HALF], U32, name="h_codes%d%d" % (t, a), align_bytes=64) for t in range(2) for a in range(2)}
        h_scales = {(t, a): sbuf.tile([P, HALF], U8, name="h_scales%d%d" % (t, a), align_bytes=64) for t in range(2) for a in range(2)}
        w_codes = sbuf.tile([P, 2, 2 * M], U8, name="w_codes", align_bytes=64)
        w_plane = sbuf.tile([P, 2, M], U8, name="w_plane", align_bytes=64)
        result = {
            (t, s): sbuf.tile([P, STORE_TILES, HALF], F32, name="result%d_%d" % (t, s), align_bytes=64)
            for t in range(2)
            for s in range(N_TILES // STORE_TILES)
        }
        identity = sbuf.tile([P, P], F32, name="identity", align_bytes=64)
        bias_rows = sbuf.tile([P, P], F32, name="bias_rows", align_bytes=64)
        bias = sbuf.tile([P, N_TILES], F32, name="bias", align_bytes=64)
        bank = [psum.tile([P, HALF], F32, name="bank%d" % s) for s in range(8)]

        pc_banks = {(0, 0): [0, 1, 2, 3], (0, 1): [0, 1, 2, 3], (1, 0): [0, 1, 2, 3], (1, 1): [4, 5, 6, 7]}

        def load(n):
            name, g, half = units[n]
            rows = dram[name][g * PASS : (g + 1) * PASS, half * HALF : (half + 1) * HALF]
            nc.sync.dma_start(out=raw[n % RAW_SLOTS][:], in_=rows.rearrange("(p j) w -> p j w", j=PACK))
            if units[n] == ("wx", 0, 1):
                nc.sync.dma_start(out=w_codes[:].bitcast(I32), in_=w_words.rearrange("a p n -> p a n").bitcast(I32))

        def cast(unit, scalar_groups):
            n = units.index(unit)
            src = raw[n % RAW_SLOTS][:].rearrange("p j (m i) -> p m j i", i=PACK)
            layout = "p (i m j) -> p m j i" if unit[0] in ("wx", "wc") else "p (m i j) -> p m j i"
            dst = grouped[n % GROUPED_SLOTS][:].rearrange(layout, i=PACK, j=PACK)
            if scalar_groups > 0:
                nc.scalar.copy(out=dst[:, :scalar_groups], in_=src[:, :scalar_groups])
            if scalar_groups < P:
                nc.vector.tensor_copy(out=dst[:, scalar_groups:], in_=src[:, scalar_groups:])
            if n + RAW_SLOTS < len(units):
                load(n + RAW_SLOTS)

        def quantize(unit):
            n = units.index(unit)
            fmt = E5M2 if unit[0] == "c" else E4M3
            nc.vector.quantize_mx(out=codes[unit][:].bitcast(fmt), scales=scales[unit][:], in_=grouped[n % GROUPED_SLOTS][:])

        def pc_pass(t, a, g, j):
            s = pc_banks[t, a][j]
            cols = slice(j * P, (j + 1) * P)
            nc.tensor.matmul_mx(
                out=bank[s][:],
                lhsT=codes["wc", g, a][:, cols].bitcast(E4M3),
                lhsT_scale=scales["wc", g, a][:, cols],
                rhs=codes["c", g, t][:].bitcast(E5M2),
                rhs_scale=scales["c", g, t][:],
                start=(g == 0),
                stop=(g == C_PASSES - 1),
            )

        def pc_copy(t, a, j, c0=0, c1=HALF):
            nc.scalar.copy(out=pc_sb[a][:, j, c0:c1], in_=bank[pc_banks[t, a][j]][:, c0:c1])

        def px(t, a, q, s):
            t_cols = slice(q * QUARTER, (q + 1) * QUARTER)
            for j in range(PACK):
                cols = slice(j * P, (j + 1) * P)
                nc.tensor.matmul_mx(
                    out=bank[s][:, j * QUARTER : (j + 1) * QUARTER],
                    lhsT=codes["wx", 0, a][:, cols].bitcast(E4M3),
                    lhsT_scale=scales["wx", 0, a][:, cols],
                    rhs=codes["x", 0, t][:, t_cols].bitcast(E4M3),
                    rhs_scale=scales["x", 0, t][:, t_cols],
                    start=True,
                    stop=True,
                )

        def multiply(a, q, s):
            t_cols = slice(q * QUARTER, (q + 1) * QUARTER)
            nc.vector.tensor_tensor(
                out=h_bf[a][:, q * PACK * QUARTER : (q + 1) * PACK * QUARTER].rearrange("p (m i j) -> p m j i", i=PACK, j=PACK),
                in0=bank[s][:].rearrange("p (j m i) -> p m j i", j=PACK, i=PACK),
                in1=pc_sb[a][:, :, t_cols].rearrange("p j (m i) -> p m j i", i=PACK),
                op=mybir.AluOpType.mult,
            )

        def quantize_h(t, a, q0, q1):
            cols = slice(q0 * QUARTER, q1 * QUARTER)
            nc.vector.quantize_mx(
                out=h_codes[t, a][:, cols].bitcast(E4M3),
                scales=h_scales[t, a][:, cols],
                in_=h_bf[a][:, q0 * PACK * QUARTER : q1 * PACK * QUARTER],
            )

        def h_quarter(t, a, q, s, whole=False):
            px(t, a, q, s)
            multiply(a, q, s)
            if q == 2 and not whole:
                quantize_h(t, a, 0, 2)
            if q == 3 and not whole:
                quantize_h(t, a, 2, 3)
                quantize_h(t, a, 3, 4)

        def pc_passes(t, a, g):
            for j in range(PACK):
                pc_pass(t, a, g, j)

        def y_pass(t, i, a, s):
            nc.tensor.matmul_mx(
                out=bank[s][:],
                lhsT=w_codes[:, a, 2 * i * P : 2 * (i + 1) * P].bitcast(E2M1),
                lhsT_scale=w_plane[:, a, i * P : (i + 1) * P],
                rhs=h_codes[t, a][:].bitcast(E4M3),
                rhs_scale=h_scales[t, a][:],
                start=(a == 0),
                stop=(a == 1),
            )

        def add_bias(t, i, s, on_vector=False):
            dst = result[t, i // STORE_TILES][:, i % STORE_TILES, :]
            if on_vector:
                nc.vector.tensor_scalar(out=dst, in0=bank[s][:], scalar1=bias[:, i : i + 1], scalar2=None, op0=mybir.AluOpType.add)
            else:
                nc.scalar.activation(out=dst, in_=bank[s][:], func=mybir.ActivationFunctionType.Identity, bias=bias[:, i : i + 1])
            if t == 1 and i >= N_TILES - STORE_TILES:
                nc.sync.dma_start(out=out[i * P : (i + 1) * P, HALF:], in_=dst)
            elif i % STORE_TILES == STORE_TILES - 1:
                s0 = i // STORE_TILES
                rows = out[s0 * STORE_TILES * P : (s0 + 1) * STORE_TILES * P, t * HALF : (t + 1) * HALF]
                nc.sync.dma_start(out=rows.rearrange("(e p) w -> p e w", p=P), in_=result[t, s0][:])

        def y_tile(t, i, s, on_vector=False):
            y_pass(t, i, 0, s)
            y_pass(t, i, 1, s)
            add_bias(t, i, s, on_vector)

        with tc.manual_schedule():
            nc.vector.memset(w_plane[:].bitcast(I32), 0)
            nc.vector.memset(bias_rows[:], 0.0)
            for n in range(3):
                load(n)
            for quad in range(4):
                nc.sync.dma_start(
                    out=w_plane[32 * quad : 32 * quad + 4].bitcast(I32),
                    in_=w_scales[:, 4 * quad : 4 * quad + 4, :].rearrange("a r n -> r a n").bitcast(I32),
                )
            nc.sync.dma_start(out=bias_rows[:N_TILES, :], in_=b.rearrange("(i p) -> i p", p=P))
            for n in range(3, RAW_SLOTS):
                load(n)
            make_identity(nc, identity[:])

            share = 48
            for g in range(C_PASSES):
                for name in ("c", "wc"):
                    cast((name, g, 0), share)
                    quantize((name, g, 0))
                if g == 2:
                    nc.tensor.transpose(bank[4][:, :P], bias_rows[:], identity[:])
                    nc.scalar.copy(out=bias[:], in_=bank[4][:, :N_TILES])
                pc_passes(0, 0, g)
            cast(("x", 0, 0), 0)
            quantize(("x", 0, 0))
            for j in range(PACK):
                pc_copy(0, 0, j)
            cast(("wx", 0, 0), share)
            quantize(("wx", 0, 0))
            cast(("wc", 0, 1), 80)
            for q in range(4):
                h_quarter(0, 0, q, 4 + q, True)
                if q == 1:
                    quantize(("wc", 0, 1))
            pc_passes(0, 1, 0)
            for g in range(1, C_PASSES):
                cast(("wc", g, 1), [0, 96, 48][g])
                quantize(("wc", g, 1))
                pc_passes(0, 1, g)
            cast(("wx", 0, 1), 48)
            quantize(("wx", 0, 1))
            quantize_h(0, 0, 0, 4)
            for c0 in (0, 256):
                for j in range(PACK):
                    pc_copy(0, 1, j, c0, c0 + 256)
            early = [4, 5, 0, 1, 2, 3, 6, 7]
            for q in range(4):
                h_quarter(0, 1, q, 6 + q % 2)
                if q > 0:
                    for i in range(2 * q - 2, 2 * q):
                        y_pass(0, i, 0, early[i])
            y_pass(0, 6, 0, 6)
            y_pass(0, 7, 0, 7)
            cast(("c", 0, 1), 128)
            cast(("c", 1, 1), 0)
            quantize(("c", 0, 1))
            quantize(("c", 1, 1))
            for i in (2, 3, 4, 5, 0, 1, 6, 7):
                y_pass(0, i, 1, early[i])
            for i in (2, 3, 4, 5):
                add_bias(0, i, early[i])
            cast(("c", 2, 1), 48)
            quantize(("c", 2, 1))
            for i in (0, 1, 6, 7):
                add_bias(0, i, early[i])
            pc_passes(1, 0, 0)
            pc_passes(1, 0, 1)
            pc_pass(1, 1, 0, 0)
            pc_passes(1, 0, 2)
            cast(("x", 0, 1), 0)
            quantize(("x", 0, 1))
            pc_copy(1, 0, 0)
            pc_copy(1, 0, 1)
            for c0 in (0, 256):
                for j in (2, 3):
                    pc_copy(1, 0, j, c0, c0 + 256)
            for j in range(PACK):
                for g in range(1 if j == 0 else 0, C_PASSES):
                    pc_pass(1, 1, g, j)
                pc_copy(1, 1, j)
                if j in (1, 2):
                    h_quarter(1, 0, 2 * j - 2, 2 * j - 2)
                    h_quarter(1, 0, 2 * j - 1, 2 * j - 1)
            for q in range(4):
                h_quarter(1, 1, q, q)
                y_tile(0, 8 + q, 4 + q)
            late = [4, 5, 0, 1, 6, 2, 7, 3]
            for i in range(3):
                y_pass(1, i, 0, late[i])
            for i in range(12):
                if i >= 3:
                    y_pass(1, i, 0, late[i % 8])
                y_pass(1, i, 1, late[i % 8])
                add_bias(1, i, late[i % 8], i % 2 == 0)
